import numpy as np, ml_dtypes
CORES = [48,51,52,55]
N = 4
import mx_ref
BF = ml_dtypes.bfloat16
def gcols(t, e):
    v = np.concatenate([t.reshape(8, 16, -1, 4), np.zeros((8, 16, 1, 4), BF)], axis=2)
    return np.ascontiguousarray(np.stack([v[g][:, e[g]] for g in range(8)])).reshape(128, -1)
def tile(rs):
    return np.stack(rs, axis=2).reshape(128, -1).astype(BF)
def pick(q, e):
    c = np.concatenate([q[0].reshape(128, -1, 4), np.zeros((128, 1, 4), np.uint8)], axis=1); s = np.concatenate([q[1], np.ones((16, 1), np.uint8)], axis=1)
    return (np.ascontiguousarray(c[:, e].reshape(128, -1)), np.ascontiguousarray(s[:, e]))
def join(*qs):
    return (np.concatenate([q[0] for q in qs], axis=1), np.concatenate([q[1] for q in qs], axis=1))
def put(q, e, v):
    c, s = q[0].reshape(128, -1, 4).copy(), q[1].copy(); c[:, e] = v[0].reshape(128, -1, 4); s[:, e] = v[1]
    return (c.reshape(128, -1), s)
def pk(c, s):
    return (np.ascontiguousarray(c), mx_ref.live(s))
def emit(q):
    return q[0], q[1]
def packed(v, rng):
    q = [mx_ref.quantize(np.ascontiguousarray(v[r])) for r in range(N)]
    return np.stack([a for a, b in q]), np.stack([mx_ref.plane(b, rng) for a, b in q])
def values_of_codes():
    e, c = np.zeros((128, 128, 4), np.float32), np.zeros((128, 2, 4), np.uint8)
    e[np.arange(128), np.arange(128), 0] = 1
    c[:127, :, 0] = np.arange(256).reshape(2, 128).T[:127]
    return mx_ref.matmul(mx_ref.quantize(e.reshape(128, 512).astype(BF)), (c.reshape(128, 8), np.full((16, 2), 127, np.uint8))).T.reshape(-1).astype(np.float64)
CODE_VALUE, SCALE_VALUE = values_of_codes(), 2.0 ** (np.arange(256) - 127.0)
def decode(q):
    return (CODE_VALUE[q[0]].reshape(16, 8, -1, 4) * SCALE_VALUE[q[1]][:, None, :, None] + 0.0).reshape(128, -1).astype(np.float32)
def f(rng, *shape):
    return mx_ref.flush((rng.standard_normal(shape, dtype=np.float32) * np.exp2(rng.integers(-2, 3, shape[:-1] + (1,)))).astype(BF))
def wide(rng, *shape, cols=0):
    v = rng.standard_normal(shape, dtype=np.float32) * np.exp2(rng.integers(-12, 13, shape)).astype(np.float32)
    if cols: v *= np.repeat(np.exp2(rng.integers(-cols, cols + 1, shape[:-2] + (1, shape[-1] // 4))) * (rng.random(shape[:-2] + (1, shape[-1] // 4)) > 0.0625), 4, axis=-1).astype(np.float32)
    return mx_ref.flush(v.astype(BF))
C, B = 320, 224
def big(v):
    v = v.astype(np.float32)
    v[np.abs(v) < np.float32(2.0 ** -16)] = 0
    return v.astype(BF)
def shared(u):
    u = np.array(u).reshape(8, 16, 8, 16, 4)
    for g in range(8): u[np.arange(8) != g, :, g, 0] = 0
    return np.repeat(u.reshape(1, 128, 512), N, axis=0)
def numbers_of(rng):
    return {"x": big(f(rng, N, 128, 4 * C)), "h": np.array(f(rng, N, 128, 4 * B)), "u": shared(f(rng, 128, 512)), "v": np.array(f(rng, N, 128, 512))}
def layers(rng, still=[]):
    w = np.array(f(rng, N, 128, 2048)).reshape(N, 8, 16, 4, 8, 16, 4)
    for i in still:
        w[:, :, i] = 0
        w[:, :, :, :, :, i] = 0
    return w
def weights(rng, w):
    c, p = packed(np.ascontiguousarray(w).reshape(N, 128, 2048), rng)
    return {"wc": c, "ws": p}
def tiles(x, h, u, v):
    return {"x": x.reshape(N, 128, 4 * C).astype(BF), "h": h.reshape(N, 128, 4 * B).astype(BF), "u": shared(u), "v": v}
def setup_inputs(rng):
    return {**numbers_of(rng), **weights(rng, layers(rng))}
def setup_inputs_ties(rng):
    d = numbers_of(rng)
    e = rng.permutation(N)
    a = (rng.integers(4, 8, (8, 8, 3, 4)) * rng.choice([-1.0, 1.0], (8, 8, 3, 4))).astype(np.float32).astype(BF)
    a[:, :, 2] = 0
    x, h = d["x"].reshape(N, 8, 16, C, 4), d["h"].reshape(N, 8, 16, B, 4)
    for r in range(N):
        for g in range(8):
            x[r, g, :8] = a[g][:, np.zeros(C, int) if r == e[0] else rng.permutation(C) % 3]
            h[r, g, :8] = a[g][:, rng.permutation(B) % 3]
    x[e[1]] = 0
    u = d["u"][0].copy().reshape(8, 16, 8, 16, 4)
    u[:, 8:, :, 0] = 0
    return {**tiles(x, h, u, d["v"]), **weights(rng, layers(rng, range(8)))}
def setup_inputs_near(rng):
    d = numbers_of(rng)
    a, c = rng.permutation(8), rng.permutation(8) % 2 * 2.0 - 1.0
    o = a % 4
    size = np.where(o == 3, 2.0 ** -6, 1.0)[:, None, None]
    x, h = d["x"].astype(np.float32).reshape(N, 8, 16, C, 4), d["h"].astype(np.float32).reshape(N, 8, 16, B, 4)
    shift = rng.integers(0, C, (N, 8, 1))
    for t, s in ((x, (np.arange(C) + shift) % C // 2), (h, np.argsort(rng.random((N, 8, B)), axis=2) * (C // 2) // (B - 1))):
        k = ((s[..., None] >> np.arange(8)) & 1) * np.exp2(np.arange(8) - 23.0) * size
        t[:, :, 0] = 0
        t[:, :, 0, :, 0] = np.where(o < 2, c, 0)[:, None]
        t[:, :, 8] = k[..., :4]
        t[:, :, 9] = k[..., 4:]
        t[:, :, 10:] = rng.integers(4, 8, (N, 8, 6, s.shape[2], 4)) * 2.0 ** -20 * size[..., None]
        t[:, :, 10, :, 0] = np.where(o < 2, 2.0 ** -16, 0)[:, None]
        t[:, :, 11, :, 0] = 2.0 ** -20 * size[..., 0]
    h[:, o == 3, 10, 1::2, 0] = 2.0 ** -30
    at = np.argsort(a)
    for r in range(N):
        for g in np.concatenate([rng.permutation(at[:4])[:2], rng.permutation(at[4:])[:2]]):
            x[r, g, 0, (C // 4 + rng.integers(C // 2) - shift[r, g, 0]) % C, 0] = rng.choice([-1.0, 1.0]) * 2.0 ** 30
    u = d["u"][0].astype(np.float32).reshape(128, 128, 4)
    u[:, ::16] = 0
    for g in range(8):
        k = 1.0 if o[g] == 0 else 2.0 ** -30
        u[16 * g, 16 * g, 0] = k
        u[16 * g + 8:16 * g + 10, 16 * g] = k
        u[16 * g + 10, 16 * g, 0] = k * (64.0 if o[g] < 2 else 1.0)
        u[16 * g + 11, 16 * g, 0] = k
    w = layers(rng, [0, 8, 9, 10, 11, 12, 13, 14, 15])
    change = np.array([0.0, -1, -2, 1])[(rng.permutation(N)[:, None] + 2 * (a // 4)) % 4]
    for g in range(8): w[:, g, 11, 0, g, 11, 0] = (4 * change[:, g]).astype(np.float32).astype(BF)
    return {**tiles(x, h, u.astype(BF), d["v"]), **weights(rng, w)}
def setup_inputs_ends(rng):
    d = numbers_of(rng)
    x, h = d["x"].astype(np.float32).reshape(N, 8, 16, C, 4), d["h"].astype(np.float32).reshape(N, 8, 16, B, 4)
    for t, s in ((x, np.argsort(rng.random((N, 8, C)), axis=2)), (h, rng.integers(0, C, (N, 8, B)))):
        z = ((s[..., None] >> np.arange(12)) & 1) * np.exp2(np.arange(12.0))
        t[:, :, 0] = 0
        for i in range(3): t[:, :, 8 + i] = z[..., 4 * i:4 * i + 4]
    k = np.stack([rng.permutation(8) for r in range(N)])
    x[:, :, 0, :, 0] = ((rng.permutation(8) < 2) * 512.0 * (np.arange(N) % 2)[:, None])[:, :, None]
    h[:, :, 0, :, 0] = np.array([-1024.0, -1024, 1024, 1024, 0, 0, 0, 0])[k][:, :, None]
    x[:, :, 4] = 0
    x[:, :, 4, :, 0] = 64
    w = layers(rng, [0, 8, 9, 10, 11, 12, 13, 14, 15])
    for g in range(8): w[:, g, 4, 0, g, 0, 0] = np.array([1024.0, 0, -1024, 0, 1024, -1024, 0, 0])[k[:, g]].astype(np.float32).astype(BF)
    u = d["u"][0].astype(np.float32).reshape(128, 128, 4)
    u[:, ::16] = 0
    for g in range(8):
        u[16 * g, 16 * g, 0] = 1
        u[16 * g + 8:16 * g + 11, 16 * g] = 1
    return {**tiles(x, h, u.astype(BF), d["v"]), **weights(rng, w)}
def setup_inputs_huge(rng):
    d = numbers_of(rng)
    k = rng.permutation(8)
    def sized(n):
        s = np.where((k < 4)[:, None, None, None], rng.choice([-1.0, 1.0], (N, 8, 1, n, 1)), 1.0)
        return ((0.7 + 0.2 * rng.random((N, 8, 1, n, 1))) * (0.95 + 0.05 * rng.random((N, 8, 16, n, 4))) * s * 2.0 ** 30).astype(np.float32)
    u = d["u"][0].astype(np.float32).reshape(8, 16, 8, 16, 4)
    u[:, :, :, 0] = 2.0 ** 30 * (1 - 0.1 * rng.random((8, 16, 8, 4))) * (k % 2 * 2.0 - 1.0)[:, None]
    w = np.zeros((N, 128, 4, 128, 4), np.float32)
    i = np.arange(128)
    for b in range(4): w[:, i, b, i, b] = -1
    return {**tiles(sized(C), sized(B), u.astype(BF), d["v"]), **weights(rng, w.astype(BF))}
def setup_inputs_spread(rng):
    d = setup_inputs(rng)
    d["x"] = big(wide(rng, N, 128, 4 * C, cols=6))
    d["h"] = wide(rng, N, 128, 4 * B)
    return d
def check_inputs(d):
    b = []
    for k in ("x", "h", "u", "v"):
        a = np.abs(d[k].astype(np.float32))
        if not (np.isfinite(a).all() and ((a == 0) | (a >= 2.0 ** -30) & (a <= 2.0 ** 30)).all()): b.append("a value of " + k)
    a = d["u"].astype(np.float32)
    if (a != a[:1]).any(): b.append("u: not the same on all ranks")
    a = a.reshape(N, 8, 16, 8, 16, 4)
    for g in range(8):
        if (a[:, np.arange(8) != g, :, g, 0] != 0).any(): b.append("u: column 16 * g outside group g")
    none, least, most = [emit(mx_ref.quantize(np.full((128, 16), k, np.float32).astype(BF)))[1][0, 0] for k in (0.0, 2.0 ** -30, 2.0 ** 30)]
    for r in range(N):
        if ((d["wc"][r] == 0x7F) | (d["wc"][r] == 0xFF)).any(): b.append("wc: a code that is no number")
        s = mx_ref.live(d["ws"][r])
        if ((s != none) & ((s < least) | (s > most))).any(): b.append("ws: a scale out of range")
    return b
def keys(qu, c):
    return mx_ref.matmul(qu, c)[::16] + np.float32(0.0)
def order(k):
    return np.argsort(k, axis=1, kind="stable")
def step(t, m, p, a, w):
    lower = gcols(t, np.take_along_axis(m, np.maximum(p - 1, 0), axis=1)).astype(np.float32)
    upper = gcols(t, np.take_along_axis(m, np.minimum(p, m.shape[1] - 1), axis=1)).astype(np.float32)
    z = mx_ref.quantize(((lower + upper) * np.float32(0.5)).astype(BF))
    d = decode(a)
    return tile([mx_ref.matmul(pick(w, np.arange(128 * b, 128 * b + 128)), z) * np.float32(0.03125) + d[:, b::4] for b in range(4)])
def reference(x, h, u, v, wc, ws):
    qu = [mx_ref.quantize(u[r]) for r in range(N)]
    lay = [pk(wc[r], ws[r]) for r in range(N)]
    k0 = [keys(qu[r], mx_ref.quantize(x[r])) for r in range(N)]
    m0 = [order(k0[r]) for r in range(N)]
    sample = [mx_ref.quantize(gcols(x[r], m0[r][:, 1::2])) for r in range(N)]
    sent, bridge = [], []
    for r in range(N):
        came = sample[(r + 1) % N]
        k1 = np.concatenate([k0[r], keys(qu[r], came)], axis=1)
        a = mx_ref.quantize(h[r])
        below = k1[:, None, :] < keys(qu[r], a)[:, :, None]
        t = np.concatenate([x[r], decode(came).astype(BF)], axis=1)
        sent.append(mx_ref.quantize(step(t, order(k1), np.sum(below, axis=2), a, lay[r])))
        bridge.append(2 * np.sum(below[:, :, C:], axis=2))
    y, ov = np.zeros((N, 128, B), np.float32), np.zeros((N, 8, B), np.float32)
    oc, osc = np.zeros((N, 128, 4 * B), np.uint8), np.zeros((N, 16, B), np.uint8)
    for r in range(N):
        a, i = sent[r - 1], np.clip(bridge[r - 1], 1, C - 1)
        s, k = keys(qu[r], a), np.take_along_axis(k0[r], m0[r], axis=1)
        p = i + (s > np.take_along_axis(k, i, axis=1)) - (s < np.take_along_axis(k, i - 1, axis=1))
        last = mx_ref.quantize(step(x[r], m0[r], p, a, lay[r]))
        y[r] = mx_ref.matmul(mx_ref.quantize(v[r]), last)
        ov[r] = p
        oc[r], osc[r] = emit(last)
    return {"y": y, "ov": ov, "oc": oc, "osc": osc}

from concourse.mybir import dt, AluOpType as A, ActivationFunctionType as F

C, B = 320, 224
NS = C // 2
SP = 336
AR = 4 * SP
BIG = 1e29
LO, NEW, BK = (0, 96), (0, 128), (4, 0)
ON_SCALAR = [10, 0, 1, 2, 3, 4, 5, 6, 7, 19, 8, 9]

f32, bf, u16, i32, cd, u8 = "float32", "bfloat16", "uint16", "int32", "float8_e4m3fn_x4", "uint8"
SCRATCH = {"ps": ("psum", [128, 4096], "float32")}


def _sb(dtype, **kw):
    for k, n in kw.items():
        SCRATCH[k] = ("sbuf", [128, n], dtype)


_sb(bf, xb=1280, hb=896, ub=512, vb=512, ef=516, ag=512, gi=32, w4=512, wg=1024, j16=112, m16=448, r16=448, j4=168, m4=168,
    r4=168, r11=160, r3=42, fr=12 * C + 192, sgn=1920, rsb=576, io2=C, wm=384, tr=704, ft=736, fa=672, lv=640,
    xh=1280, dh=1280, xt=8 * SP, zt=4 * SP, ut=896, z1=896, y1=896, z2=896, y2=896)
_sb(cd, qx=C, qh=B, qu=128, qr=128, qv=128, wq=512, lx=C, ly=B, qe=512, q4=128, qg=256, qf=1008, qo=184, qa=168, qz1=256,
    qy1=256, qz2=256, qy2=256)
_sb(u8, sx=C, sh=B, su=128, sr=128, sv=128, wp=512, lxs=C, lys=B, se=512, s4=128, sg=256, sf=1008, so=184, sa=168, sz1=256,
    sy1=256, sz2=256, sy2=256)
_sb(f32, col=16, ce=2, jj=48, iot=336, ks=C, kp=C, ss=B, mk=336, sc=336, mk2=176, sq=B, srp=160, rs=20, wr=20,
    cm=168, cs=168, rk=32, kr=C + 2, ka=176, wo=352, wa=176, kl=448, bb=28, dd=28, cx=56,
    av=16, s2=14, la=14, ls=14, bm=16, g2=C, g3=448, g4=448, ff=42, fp=42, ovr=B, yo=B)
_sb(i32, pi=8, qi=10)
_sb(u16, ou=8, ot=2, ow=12, osr=10, op1=10, op2=10, ork=20, mo=16, me=16, lm=10, ob1=14, ob2=14, oo=28, oe=2, oc1=28, obr=28,
    opp=14)

_DMAS = (["x", "u", "h", "w", "ws", "v", "z1", "ov", "oc0", "oc1", "y0", "y1"] + ["j%d" % k for k in range(6)]
         + [k + str(b) for k in ("z0", "zc", "o0", "o1") for b in range(4)])
SEMAPHORES = ["cv", "cs", "ct", "cg", "sent", "ax", "am", "ab", "ay0", "az0", "as0", "ay1", "az1", "as1"] + ["d" + k for k in _DMAS]


def rank_program(g, core, T, topo):
    rank = T.rank_of(core)
    if rank is None:
        return
    n = len(T.cores)
    prv, nxt = T.cores[(rank - 1) % n], T.cores[(rank + 1) % n]
    Q = {"v": g.vector, "s": g.scalar, "t": g.tensor, "g": g, "y": g.sync}
    V, S, PE = g.vector, g.scalar, g.tensor
    cnt = {"v": 0, "s": 0, "t": 0, "g": 0}
    seen = {q: {} for q in Q}
    wr, rd, bank, sent, dmas = {}, {}, {}, [0], []

    def wait(q, ev):
        if seen[q].get(ev[0], 0) < ev[1]:
            Q[q].wait_ge(T.sem[ev[0]], ev[1])
            seen[q][ev[0]] = ev[1]

    def before(q, r, w, p):
        need = {}
        evs = [e for k in r for e in wr[k]] + [e for k in w for e in wr.get(k, []) + rd.get(k, [])]
        evs += [e for k in p for (o, e) in bank.get(k, {}).items() if o != q]
        for s, v in evs:
            need[s] = max(need.get(s, 0), v)
        for s in need:
            wait(q, (s, need[s]))

    def after(q, ev, r, w, p):
        for k in r:
            rd.setdefault(k, []).append(ev)
        for k in w:
            wr[k], rd[k] = [ev], []
        for k in p:
            bank.setdefault(k, {})[q] = ev

    def op(q, fn, r="", w="", p=""):
        r, w, p = r.split(), w.split(), p.split()
        before(q, r, w, p)
        cnt[q] += 1
        fn().then_inc(T.sem["c" + q], 1)
        after(q, ("c" + q, cnt[q]), r, w, p)

    def dma(q, name, out, in_, r="", w="", **kw):
        r, w = r.split(), w.split()
        before(q, r, w, [])
        Q[q].dma_start(out, in_, **kw).then_inc(T.sem["d" + name], 16)
        after(q, ("d" + name, 16), r, w, [])
        dmas.append("d" + name)

    def send(dst, out, in_, sem, eng, r):
        before("g", r.split(), [], [])
        rid, pid = topo.addr(dst)[:2]
        g.remote_dma(out, in_, T.sem[sem], T.sem.sent, pid, rid, sum(1 << e for e in eng))
        sent[0] += len(eng)

    def ts(out, in0, a, o0, b=None, o1=None, r="", w="", p=""):
        if o1 is None:
            op("v", lambda: V.tensor_scalar(out, in0, a, None, o0), r, w, p)
        else:
            op("v", lambda: V.tensor_scalar(out, in0, a, b, o0, o1), r, w, p)

    def tt(out, a, b, o, r="", w="", p=""):
        op("v", lambda: V.tensor_tensor(out, a, b, o), r, w, p)

    def cp(out, a, r="", w="", p=""):
        op("v", lambda: V.tensor_copy(out, a), r, w, p)

    def ms(out, c, w):
        op("v", lambda: V.memset(out, c), "", w)

    def hold(out, keep, data, r="", w="", first=0.0):
        op("v", lambda: V.tensor_tensor_scan(out, keep, data, first, A.mult, A.add), r, w)

    def act(out, a, r="", w="", p="", f=F.Copy, **kw):
        op("s", lambda: S.activation(out, a, f, **kw), r, w, p)

    def fill(out, m, c, w):
        act(out, T.fr[:, 12 * C:12 * C + m], "frpad", w, f=F.Identity, scale=0.0, bias=c)

    def qz(q, s, a, r="", w=""):
        op("v", lambda: V.quantize_mx(q, s, a), r, w)

    def P(k, a, b):
        return T.ps[:, 512 * k + a:512 * k + b]

    def mm(k, m, lq, ls, rq, rs_, r, start=True, stop=True):
        op("t", lambda: PE.matmul_mx(P(k, 0, m), lq, ls, rq, rs_, start, stop), r, "", "p%d" % k)

    def raw(v):
        return v.bitcast(dt.uint8)

    def iota(out, pat, base, cm, w, small=True):
        if small:
            op("g", lambda: g.iota(out, pat, base, cm, allow_small_or_imprecise_dtypes=True), "", w)
        else:
            op("g", lambda: g.iota(out, pat, base, cm), "", w)

    def E(b):
        return T.qe[:, 128 * b:128 * b + 128], T.se[:, 128 * b:128 * b + 128]

    ep, en = topo.engines(core, prv), topo.engines(core, nxt)
    wr["lx"] = [("ax", len(topo.engines(nxt, core)))]
    wr["lm"] = [("am", len(topo.engines(nxt, core)))]
    nb = len(topo.engines(prv, core))
    wr["la"] = [("ab", nb)]
    for k in "01":
        wr["ly" + k], wr["lys" + k], wr["ls" + k] = [("ay" + k, nb // 2)], [("az" + k, nb // 2)], [("as" + k, nb // 2)]

    dma("y", "x", T.xb[:], T.x[:], w="xb")
    dma("s", "u", T.ub[:], T.u[:], w="ub")
    dma("y", "h", T.hb[:], T.h[:], w="hb")

    JA, JB, JC, JD = [T.jj[:, 12 * k:12 * k + 10] for k in range(4)]
    iota(T.pi[:, 0:1], [[0, 1]], 0, 1, "p", False)
    iota(T.gi[:], [[1, 8], [0, 4]], 0, 0, "gi")
    iota(JA, [[16, 10]], 0, 0, "ja")
    iota(T.j16[:], [[0, 7], [1, 16]], 0, 0, "j16")
    iota(T.jj[:, 36:48], [[15, 12]], 0, 0, "jd")
    iota(T.j4[:], [[0, 42], [1, 4]], 0, 0, "j4")
    ms(T.fr[:, 12 * C:12 * C + 192], 0.0, "frpad")
    ms(T.ag[:], 255.0, "ag")
    fill(T.r11[:], 160, 1.0, "r11")
    fill(T.r3[:], 42, 1.0, "r3")
    fill(T.kr[:, 0:1], 1, -2 * BIG, "kr0")
    fill(T.kr[:, C + 1:C + 2], 1, BIG, "kr1")
    fill(T.wo[:, NS:176], 16, BIG, "wo1")
    fill(T.wo[:, 176 + NS:352], 16, BIG, "we1")
    fill(T.r11[:, 0:160:11], 15, 0.0, "r11")
    fill(T.r3[:, 0:42:3], 14, 0.0, "r3")
    fill(T.ka[:, 0:1], 1, -4 * BIG, "ka0")
    fill(T.ka[:, NS + 1:176], 15, BIG, "ka1")
    fill(T.wm[:, 0:32], 32, 0.0, "wm0")
    fill(T.wm[:, 352:384], 32, 0.0, "wm1")
    ts(T.pi[:, 1:2], T.pi[:, 0:1], 15, A.bitwise_and, r="p", w="p1")
    ts(T.pi[:, 2:3], T.pi[:, 0:1], 4, A.logical_shift_right, r="p", w="p2")
    ts(T.pi[:, 3:4], T.pi[:, 0:1], 2, A.logical_shift_right, 3, A.bitwise_and, r="p", w="p3")
    for k in range(4):
        cp(T.ag[:, 5 * k:512:16], T.gi[:], "gi ag", "ag%d" % k)
    cp(T.col[:, 0:4], T.pi[:, 0:4], "p p1 p2 p3", "col")
    rc, gc_, r4c = T.col[:, 1:2], T.col[:, 2:3], T.col[:, 3:4]
    cp(T.ou[:], T.jj[:, 0:8], "ja", "ou")
    ts(T.w4[:], T.ag[:], gc_, A.is_equal, r="ag0 ag1 ag2 ag3 col", w="w4")
    ts(T.m16[:, 0:112], T.j16[:], rc, A.is_equal, r="j16 col", w="m16a")
    op("g", lambda: g.affine_select(T.wg[:, 0:512], T.w4[:], [[1, 128], [0, 4]], A.is_gt, 0.0, 0, -1), "w4", "wg0")
    op("g", lambda: g.affine_select(T.wg[:, 512:1024], T.w4[:], [[-1, 128], [0, 4]], A.is_gt, 0.0, 0, 1), "w4", "wg1")
    act(T.col[:, 7:8], rc, "col", "cd", f=F.Sign)
    act(T.col[:, 4:5], rc, "col", "ca", f=F.Relu, scale=-float(AR - 1), bias=float(AR - 1))
    act(JB, JA, "ja col", "jb", f=F.Identity, bias=rc)
    act(T.col[:, 5:6], T.col[:, 7:8], "cd", "cb", scale=float(AR + NS - 1 - C))
    act(JC, JB, "jb", "jc", f=F.Identity, scale=1.0 / 11, bias=-5.0 / 11)
    act(T.m16[:, 112:224], T.m16[:, 0:112], "m16a", "m16b")
    act(T.col[:, 6:7], T.col[:, 7:8], "cd", "cc", f=F.Identity, scale=float(C - 1), bias=1.0)
    act(T.m16[:, 224:448], T.m16[:, 0:224], "m16a m16b", "m16")
    act(T.r16[:], T.m16[:], "m16", "r16", f=F.Identity, scale=-1.0, bias=1.0)
    ms(T.mk[:, C:336], 0.0, "mkpad")
    ms(T.fr[:, 0:160], 0.0, "frhead")
    qz(T.q4[:], T.s4[:], T.w4[:], "w4", "q4")
    ms(T.ef[:], 32.0, "ef")
    tt(T.pi[:, 4:5], T.pi[:, 1:2], T.pi[:, 2:3], A.add, "p1 p2", "p4")
    ts(T.col[:, 11:12], rc, 10.0, A.min, 16.0, A.mult, r="col", w="c11")
    ts(T.pi[:, 4:5], T.pi[:, 4:5], 1, A.bitwise_and, w="p4")
    cp(T.qi[:], JC, "jc", "qi")
    ts(T.ot[:, 0:1], T.pi[:, 4:5], 176.0, A.mult, T.col[:, 11:12], A.add, r="p4 c11", w="ot")
    ts(JA, T.qi[:], -11.0, A.mult, r="qi", w="ja")
    ts(T.ow[:], T.jj[:, 36:48], rc, A.add, r="jd col", w="ow")
    ts(T.qi[:], T.qi[:], 13.0, A.min, 16.0, A.mult, w="qi")
    tt(JA, JA, JB, A.add, "jb", "ja")

    qz(T.qu[:], T.su[:], T.ub[:], "ub", "qu")
    act(T.sr[:], T.su[:].indirect(T.ou[:]), "qu ou", "sr")
    ts(T.osr[:], T.qi[:], 15.0, A.add, r="qi", w="osr")
    cp(T.qr[:].bitcast(dt.uint32), T.qu[:].bitcast(dt.uint32).indirect(T.ou[:]), "qu ou", "qr")
    ts(JC, JA, 32.0, A.mult, 32.0, A.add, r="ja", w="jc")
    ts(T.op1[:], JA, 15.0, A.mult, 15.0, A.add, r="ja", w="op1")
    ts(T.op2[:], JC, float(C + 1), A.min, r="jc", w="op2")
    qz(T.qx[:], T.sx[:], T.xb[:], "xb", "qx")
    mm(0, C, T.qr[:], T.sr[:], T.qx[:], T.sx[:], "qr sr qx")
    mm(1, C, T.qr[:], T.sr[:], T.qx[:], T.sx[:], "qr sr qx")
    send(prv, raw(T.lx[:]), raw(T.qx[:]), "ax", ep[0::2], "qx")
    send(prv, T.lxs[:], T.sx[:], "ax", ep[1::2], "qx")
    op("g", lambda: g.affine_select(T.ef[:], T.ef[:], [[1, 516]], A.is_equal, 0.0, -3, -4), "", "ef")
    iota(T.io2[:], [[1, C]], -NS, 0, "io2")
    iota(T.iot[:], [[1, 336]], 0, 0, "iot")
    dma("y", "w", raw(T.wq[:]), T.wc[:], r="xb", w="wq")
    dma("y", "ws", T.wp[:], T.ws[:], w="wp")
    dma("y", "v", T.vb[:], T.v[:], w="vb")
    dma("y", "j0", T.xt[:, 0:1280], T.x[:], r="hb", w="xj0")
    dma("y", "j1", T.xt[:, 1280:2560], T.x[:], w="xj1")
    dma("y", "j2", T.xt[:, 2560:8 * SP], T.x[:, 0:8 * SP - 2560], w="xj2")
    dma("y", "j3", T.ft[:, 448:736], T.x[:, 0:288], w="ftpad")
    dma("y", "j4", T.zt[:, 0:1280], T.x[:], w="zj0")
    dma("y", "j5", T.zt[:, 1280:AR], T.x[:, 0:AR - 1280], w="zj1")
    for b in range(3):
        act(T.xh[:, C * b:C * b + C], T.xb[:, b:1280:4], "xb", "xh%d" % b, scale=0.5)
    qz(T.qg[:], T.sg[:], T.wg[:], "wg0 wg1", "qg")

    tt(T.mk[:, 0:176], P(0, 0, 176), T.m16[:, 0:176], A.mult, "m16", "mk", "p0")
    hold(T.sc[:, 0:176], T.r16[:, 0:176], T.mk[:, 0:176], "r16 mk", "sca")
    tt(T.mk[:, 176:C], P(0, 176, C), T.m16[:, 176:C], A.mult, "m16", "mkb", "p0")
    hold(T.sc[:, 176:336], T.r16[:, 176:336], T.mk[:, 176:336], "r16 mkb mkpad sca", "sc", T.sc[:, 175:176])

    def at(f):
        return (9 - f) * C

    def pivot(c):
        k = T.sc[:, 16 * c + 15:16 * c + 16]
        if c in ON_SCALAR:
            width = 160 if c < 10 else 144
            h = ON_SCALAR.index(c)
            tmp, nm = T.sgn[:, 160 * h:160 * h + width], "sgn%d" % h
            if c < 19:
                lo = at(c % 10) + 16 * c + 16
                act(tmp, P(1, 16 * c + 16, 16 * c + 16 + width), "sca", nm, "p1", f=F.Sign, scale=-1.0, bias=k)
                return lambda: act(T.fr[:, lo:lo + width], tmp, nm, "f%d rs%d" % (c, c), f=F.Sign, scale=-1.0, bias=1.0,
                                   accum_out=T.rs[:, c:c + 1])
            act(tmp, P(1, 0, 144), "sc", nm, "p1", f=F.Sign, scale=-1.0, bias=k)
            return lambda: act(T.fr[:, C:C + 144], tmp, nm, "h19 rs19", f=F.Relu, scale=-1.0, accum_out=T.rs[:, c:c + 1])
        f = c - 10
        lo = at(f) + 16 * c + 16
        ts(T.fr[:, lo:at(f) + C], P(0, 16 * c + 16, C), k, A.is_ge, r="sc", w="f%d" % c, p="p0")
        ts(T.fr[:, at(f) + C:at(f) + C + 16 * f], P(0, 0, 16 * f), k, A.is_gt, r="sc", w="h%d" % c, p="p0")
        return lambda: op("v", lambda: V.tensor_tensor_scan(T.rsb[:, 72 * (c - 11):72 * (c - 10)], T.fr[:, lo:lo + 72],
                                                            T.fr[:, lo + 72:lo + 144], 0.0, A.add, A.add),
                          "f%d h%d" % (c, c), "rs%d" % c)

    def frames(f, last):
        a = (8 - f) * 80
        r = " ".join("f%d f%d h%d" % (k, k + 10, k + 11) for k in (f, f + 1)) + " frhead"
        r = " ".join(k for k in r.split() if k in wr)
        qz(T.qf[:, a:a + 160], T.sf[:, a:a + 160], T.fr[:, 4 * a:4 * a + 640], r, "qf%d" % f)
        mm(3, 128, T.q4[:], T.s4[:], T.qf[:, a + 80:a + 208], T.sf[:, a + 80:a + 208],
           "q4 qfd qf%d" % f + (" qf%d" % (f - 2) if f else ""), False, False)
        mm(3, 128, T.q4[:], T.s4[:], T.qf[:, a:a + 128], T.sf[:, a:a + 128], "q4 qf%d" % f, False, last)

    tail = pivot(ON_SCALAR[0])
    for c in ON_SCALAR[1:]:
        nx_ = pivot(c)
        tail()
        tail = nx_
    tail()
    tt(T.fr[:, 10 * C:11 * C], P(0, 0, C), T.sc[:, 0:C], A.is_ge, "sc", "fd0", "p0")
    tt(T.fr[:, 11 * C:12 * C], P(0, 0, C), T.sc[:, 16:336], A.is_gt, "sc", "fd1", "p0")
    tail = pivot(11)
    qz(T.qf[:, 800:1008], T.sf[:, 800:1008], T.fr[:, 3200:4032], "fd0 fd1 frpad", "qfd")
    mm(3, 128, T.qg[:, 0:128], T.sg[:, 0:128], T.qf[:, 800:928], T.sf[:, 800:928], "qg qfd", True, False)
    mm(3, 128, T.qg[:, 128:256], T.sg[:, 128:256], T.qf[:, 880:1008], T.sf[:, 880:1008], "qg qfd", False, False)
    for c in range(12, 19):
        nx_ = pivot(c)
        tail()
        tail = nx_
        if c in (13, 15, 17):
            frames(c - 13, False)
    tail()
    qz(T.qh[:], T.sh[:], T.hb[:], "hb", "qh")
    mm(2, B, T.qr[:], T.sr[:], T.qh[:], T.sh[:], "qr sr qh")
    frames(6, False)
    ts(T.m4[:], T.j4[:], r4c, A.is_equal, r="j4 col", w="m4")
    for b in range(3):
        qz(*E(b), T.ef[:, 3 - b:515 - b], "ef", "qe%d" % b)
    frames(8, True)
    tt(T.mk[:, 0:B], P(2, 0, B), T.m16[:, 0:B], A.mult, "m16", "mk mkb", "p2")
    qz(*E(3), T.ef[:, 0:512], "ef", "qe3")
    act(T.r4[:], T.m4[:], "m4", "r4", f=F.Identity, scale=-1.0, bias=1.0)
    act(T.wr[:, 11:19], T.rsb[:, 71:576:72], " ".join("rs%d" % c for c in range(11, 19)), "wr1", f=F.Identity, scale=-1.0, bias=144.0)
    act(T.wr[:, 0:10], T.rs[:, 0:10], " ".join("rs%d" % c for c in range(10)), "wr0", f=F.Identity, scale=-1.0, bias=160.0)
    act(T.wr[:, 10:20:9], T.rs[:, 10:20:9], "rs10 rs19", "wr2", f=F.Identity, scale=-1.0, bias=144.0)
    tt(T.cm[:, 0:80], P(3, 0, 80), T.m4[:, 0:80], A.mult, "m4", "cm", "p3")
    hold(T.cs[:, 0:80], T.r4[:, 0:80], T.cm[:, 0:80], "r4 cm", "cs")
    tt(T.rk[:, 0:20], T.cs[:, 3:80:4], T.wr[:], A.add, "cs wr0 wr1 wr2", "rk")
    cp(T.ork[:], T.rk[:, 0:20], "rk", "ork")
    cp(T.wm[:, 32:352].indirect(T.ork[:]), T.io2[:], "ork io2", "wm")

    def places(o, base, out, nm):
        op("v", lambda: V.transpose(T.tr[:, base:base + 160], T.wm[:, 32 + o:352:2]), "wm", nm + "a")
        op("v", lambda: V.transpose(T.tr[:, base + 160:base + 352], T.wm[:, o:384:2]), "wm wm0 wm1", nm + "b")
        ts(out, T.tr[:, base:base + 352].indirect(T.ot[:, 0:1]), float(NS), A.add, r="ot %sa %sb" % (nm, nm), w=nm)

    places(1, 0, T.mo[:], "mo")
    MO, ME = T.mo[:, 0:10], T.me[:, 0:10]
    send(prv, T.lm[:], MO, "am", ep, "mo")

    mm(0, C, T.qr[:], T.sr[:], T.lx[:], T.lxs[:], "qr sr lx")
    act(T.ks[:], P(1, 0, C), "", "ks", "p1")
    act(T.xh[:, 3 * C:4 * C], T.xb[:, 3:1280:4], "xb", "xh3", scale=0.5)
    act(T.ss[:], P(2, 0, B), "", "ss", "p2")
    act(T.kp[:], P(0, 0, C), "", "kp", "p0")
    for b in range(4):
        mm(4 + b, C, *E(b), T.lx[:], T.lxs[:], "qe%d lx" % b)
    for b in range(4):
        act(T.dh[:, C * b:C * b + C], P(4 + b, 0, C), "", "dh%d" % b, "p%d" % (4 + b), scale=1.0 / 64)
        mm(4 + b, 128, *E(b), T.qh[:, 0:128], T.sh[:, 0:128], "qe%d qh" % b, True, False)
    act(T.kr[:, 2:C + 2:2], T.ks[:].indirect(MO), "ks mo", "kro")

    def table(b):
        for (o, nm, lst) in ((2, "mo", MO), (1, "me", ME)):
            act(T.xt[:, SP * b + o:SP * b + o + C:2], T.xh[:, C * b:C * b + C].indirect(lst), "xh%d %s xj0 xj1 xj2" % (b, nm), "xo%d%s" % (b, nm))
        own = "xo%dmo xo%dme" % (b, b)
        dma("y", "z0%d" % b, T.zt[:, SP * b + 1:SP * b + C], T.xt[:, SP * b + 1:SP * b + C], r=own + " zj0 zj1", w="zt%d" % b)
        dma("y", "zc%d" % b, T.fr[:, SP * b + 1:SP * b + C], T.xt[:, SP * b + 2:SP * b + C + 1], r=own + " qf8", w="zc%d" % b)

    places(0, 352, T.me[:], "me")
    hold(T.sq[:], T.r16[:, 0:B], T.mk[:, 0:B], "r16 mk", "sq")
    act(T.kr[:, 1:C + 1:2], T.ks[:].indirect(ME), "ks me kro", "kre")
    act(T.srp[:], T.sq[:].indirect(T.osr[:]), "sq osr", "srp")
    tt(T.g2[:, 0:NS], T.ks[:].indirect(MO), T.m16[:, 0:NS], A.mult, "ks mo m16", "g2a")
    tt(T.g2[:, NS:C], T.ks[:].indirect(ME), T.m16[:, 0:NS], A.mult, "ks me m16", "g2b")
    hold(T.wo[:, 0:NS], T.r16[:, 0:NS], T.g2[:, 0:NS], "r16 g2a", "wo")
    L0, L1, L2, L3 = [T.lv[:, 160 * k:160 * k + 160] for k in range(4)]
    B1, B3 = T.lv[:, 170:314:11], T.lv[:, 490:634:11]
    KR = "kro kre kr0 kr1"
    tt(L0, T.kr[:].indirect(T.op2[:]), T.srp[:], A.is_lt, KR + " op2 srp", "l0")
    hold(T.wo[:, 176:176 + NS], T.r16[:, 0:NS], T.g2[:, NS:C], "r16 g2b", "we")
    hold(L1, T.r11[:], L0, "r11 l0", "l1")
    ts(T.ob1[:], B1, 16.0, A.mult, 15.0, A.add, r="l1", w="ob1")
    tt(T.ft[:, 0:B], T.wo[:, 0:176].indirect(T.ob1[:]), T.ss[:], A.is_lt, "wo wo1 ob1 ss", "fo")
    tt(T.ft[:, B:2 * B], T.wo[:, 176:352].indirect(T.ob1[:]), T.ss[:], A.is_lt, "we we1 ob1 ss", "fe")
    table(0)
    act(T.rk[:, 0:14], B1, "l1", "rk", scale=32.0)
    table(1)
    act(T.ka[:, 1:NS + 1], T.kp[:].indirect(T.lm[:]), "kp lm", "kas")
    qz(T.qo[:], T.so[:], T.ft[:], "fo fe ftpad", "qo")
    mm(3, 128, T.q4[:], T.s4[:], T.qo[:, 0:128], T.so[:, 0:128], "q4 qo", True, False)
    mm(3, 128, T.q4[:], T.s4[:], T.qo[:, 56:184], T.so[:, 56:184], "q4 qo", False, True)
    table(2)
    table(3)

    KA = "kas ka0 ka1"
    tt(L2, T.ka[:].indirect(T.op1[:]), T.srp[:], A.is_lt, KA + " op1 srp", "l2")
    O = T.wr[:, 0:14]
    tt(T.cm[:, 0:56], P(3, 0, 56), T.m4[:, 0:56], A.mult, "m4", "cm", "p3")
    tt(T.mk2[:], T.ka[:].indirect(T.ow[:, 0:11]), T.m16[:, 0:176], A.mult, KA + " ow m16", "mk2")
    hold(T.cs[:, 0:56], T.r4[:, 0:56], T.cm[:, 0:56], "r4 cm", "cs")
    hold(L3, T.r11[:], L2, "r11 l2", "l3")
    tt(O, T.cs[:, 3:56:4], T.rk[:, 0:14], A.add, "cs rk", "wr0 wr1 wr2")
    hold(T.wa[:], T.r16[:, 0:176], T.mk2[:], "r16 mk2", "wa")
    ts(T.oo[:, 0:14], O, 0.0, A.add, r="wr0", w="oo0")
    ts(T.oo[:, 14:28], O, 1.0, A.add, r="wr0", w="oo1")
    ts(T.ob2[:], B3, 16.0, A.mult, 15.0, A.add, r="l3", w="ob2")
    act(T.kl[:, 0:B], T.kr[:].indirect(T.oo[:, 0:14]), KR + " oo0", "klo")
    act(T.kl[:, B:2 * B], T.kr[:].indirect(T.oo[:, 14:28]), KR + " oo1", "khi")
    act(T.rk[:, 0:14], B3, "l3", "rk", f=F.Identity, scale=15.0, bias=-1.0)
    act(T.rk[:, 16:30], B3, "l3", "rk2", f=F.Identity, scale=15.0, bias=float(AR - 2))
    act(T.bb[:, 0:14], O, "wr0", "bb0")
    act(T.bb[:, 14:28], O, "wr0", "bb1", f=F.Identity, bias=1.0)
    WA = T.wa[:].indirect(T.ob2[:])
    tt(T.fa[:, B:2 * B], WA, T.ss[:], A.is_lt, "wa ob2 ss", "fa0")
    tt(T.fa[:, 0:B], WA, T.kl[:, 0:B], A.is_lt, "wa ob2 klo", "fa1")
    tt(T.fa[:, 2 * B:3 * B], WA, T.kl[:, B:2 * B], A.is_lt, "wa ob2 khi", "fa2")
    qz(T.qa[:], T.sa[:], T.fa[:], "fa0 fa1 fa2", "qa")
    mm(2, 168, T.q4[:], T.s4[:], T.qa[:], T.sa[:], "q4 qa")
    ts(T.ce[:, 0:1], T.ka[:, 1:2], T.kr[:, 1:2], A.is_lt, T.col[:, 4:5], A.mult, r="kas kre ca", w="e0")
    ts(T.ce[:, 1:2], T.ka[:, NS:NS + 1], T.kr[:, C:C + 1], A.is_ge, T.col[:, 5:6], A.mult, r="kas kro cb", w="e1")
    tt(T.cx[:, 0:14], T.rk[:, 16:30], O, A.subtract, "rk2 wr0", "cx")
    ts(T.oe[:, 0:1], T.ce[:, 0:1], T.ce[:, 1:2], A.add, T.col[:, 6:7], A.add, r="e0 e1 cc", w="oe")

    for b in range(4):
        act(T.xt[:, AR + SP * b:AR + SP * b + NS], T.dh[:, C * b:C * b + C].indirect(T.lm[:]), "dh%d lm xj1 xj2" % b, "xa%d" % b)
    tab = " ".join("xo%d%s" % (b, nm) for b in range(4) for nm in ("mo", "me")) + " xa0 xa1 xa2 xa3"
    for b in (3, 2, 1, 0):
        a = SP * b + AR + NS
        act(T.xt[:, a:a + 16], T.xt[:, SP * b:a].indirect(T.oe[:, 0:1]), tab + " oe", "xs%d" % b)
        tab += " xs%d" % b
    act(T.xt[:, 0:AR:SP], T.xt[:, AR + NS:2 * AR:SP], tab, "xd0")
    act(T.xt[:, C + 1:AR:SP], T.xt[:, AR + NS + 1:2 * AR:SP], tab, "xd1")
    tab += " xd0 xd1"

    CF, CX = T.cx[:, 28:56], T.cx[:, 0:28]
    tt(T.cm[:], P(2, 0, 168), T.m4[:], A.mult, "m4", "cm", "p2")
    hold(T.cs[:], T.r4[:], T.cm[:], "r4 cm", "cs")
    C0 = T.cs[:, 59:112:4]
    tt(CF, T.cs[:, 3:112:4], T.cs[:, 59:168:4], A.is_lt, "cs", "cf")
    tt(T.dd[:, 0:14], C0, T.cx[:, 0:14], A.add, "cs cx", "dd")
    AV = T.av[:, 0:14]
    tt(AV, C0, T.rk[:, 0:14], A.add, "cs rk", "av")
    tt(T.cx[:, 0:14], T.cx[:, 28:42], T.dd[:, 0:14], A.mult, "cf dd", "cx")
    tt(T.cx[:, 14:28], T.cx[:, 42:56], T.dd[:, 0:14], A.mult, "cf dd", "cy")
    tt(T.dd[:], CX, T.bb[:], A.add, "cx cy bb0 bb1", "dd")
    cp(T.oc1[:], T.dd[:], "dd", "oc1")
    send(nxt, T.la[:], AV, "ab", en, "av")
    dma("g", "z1", T.zt[:, 0:AR - 1], T.fr[:, 0:AR - 1], r="zc0 zc1 zc2 zc3 zt0 zt1 zt2 zt3", w="zt", accum_op=A.add)

    def zgather(k, b):
        win, a, e = T.xt[:, SP * b:SP * b + AR + NS], NEW[k], LO[k] + 128
        ut, nm = T.ut[:, B * b + a:B * b + e], "ut%d%d" % (k, b)
        act(ut, win.indirect(T.oc1[:, 14 + a // 16:14 + e // 16]), tab + " oc1", nm)
        return lambda: tt(T.z1[:, 4 * a + b:4 * e:4], win.indirect(T.oc1[:, a // 16:e // 16]), ut, A.add, tab + " oc1 " + nm, "z1%d%d" % (k, b))

    def half(nm, k):
        return T["q" + nm][:, 128 * k:128 * k + 128], T["s" + nm][:, 128 * k:128 * k + 128]

    def pack(nm, k):
        qz(*half(nm, k), T[nm][:, 4 * LO[k]:4 * LO[k] + 512], " ".join("%s%d%d" % (nm, j, b) for j in range(k + 1) for b in range(4)), "q%s%d" % (nm, k))

    def layer(z, k):
        pack(z, k)
        for b in (0, 2, 1, 3):
            mm(BK[k] + b, 128, T.wq[:, 128 * b:128 * b + 128], T.wp[:, 128 * b:128 * b + 128], *half(z, k), "wq wp q%s%d" % (z, k), False, True)

    def combine(y, k, bs):
        for b in bs:
            src, out, p = P(BK[k] + b, NEW[k] - LO[k], 128), T[y][:, 4 * NEW[k] + b:4 * LO[k] + 512:4], "p%d" % (BK[k] + b)
            if b < 2:
                act(out, src, "", "%s%d%d" % (y, k, b), p, scale=0.03125)
            else:
                ts(out, src, 0.03125, A.mult, w="%s%d%d" % (y, k, b), p=p)

    def hand_on(k):
        a, e, o = NEW[k], LO[k] + 128, 128 * k + NEW[k] - LO[k]
        pack("y1", k)
        mm(BK[k], 128, T.qr[:], T.sr[:], *half("y1", k), "qr sr qy1%d" % k)
        send(nxt, raw(T.ly[:, a:e]), raw(T.qy1[:, o:128 * k + 128]), "ay%d" % k, en[0::2], "qy1%d" % k)

    def scores(k):
        a, e, o, m, s = NEW[k], LO[k] + 128, 128 * k + NEW[k] - LO[k], ("mk", "mkb")[k], ("sq", "sqb")[k]
        tt(T.mk[:, a:e], P(BK[k], a - LO[k], 128), T.m16[:, a:e], A.mult, "m16", m, "p%d" % BK[k])
        hold(T.sq[:, a:e], T.r16[:, a:e], T.mk[:, a:e], "r16 " + m, s)
        cp(T.s2[:, a // 16:e // 16], T.sq[:, a + 15:e:16], s, "s2%d" % k)
        send(nxt, T.ls[:, a // 16:e // 16], T.s2[:, a // 16:e // 16], "as%d" % k, en[1::2], "s2%d" % k)
        send(nxt, T.lys[:, a:e], T.sy1[:, o:128 * k + 128], "az%d" % k, en[1::2], "qy1%d" % k)

    for b in range(4):
        mm(b, 128, *E(b), T.qh[:, 96:B], T.sh[:, 96:B], "qe%d qh" % b, True, False)
    wr["mkb"], wr["sqb"], rd["mkb"], rd["sqb"] = list(wr["mk"]), list(wr["sq"]), list(rd["mk"]), list(rd["sq"])
    for b in range(4):
        zgather(0, b)()
    layer("z1", 0)
    zb = [zgather(1, 0), zgather(1, 1)]
    combine("y1", 0, (0,))
    zb.append(zgather(1, 2))
    combine("y1", 0, (1,))
    zb.append(zgather(1, 3))
    zb[0]()
    zb[1]()
    combine("y1", 0, (2, 3))
    hand_on(0)
    zb[2]()
    zb[3]()
    layer("z1", 1)
    scores(0)
    combine("y1", 1, (0, 2, 1, 3))
    hand_on(1)
    qz(T.qv[:], T.sv[:], T.vb[:], "vb", "qv")
    BM = T.bm[:, 0:14]
    ts(BM, T.la[:], 2.0, A.mult, 1.0, A.max, r="la", w="bm")
    act(T.zt[:, 0:AR:SP], T.xt[:, 1:AR:SP], tab + " zt", "ze0", scale=2.0)
    act(T.zt[:, C:AR:SP], T.xt[:, C:AR:SP], tab + " zt", "ze1", scale=2.0)
    scores(1)

    ts(T.obr[:, 0:14], BM, float(C - 1), A.min, r="bm", w="obr0")
    ts(T.obr[:, 14:28], BM, float(C - 1), A.min, 1.0, A.add, r="bm", w="obr1")
    ts(T.ff[:, 0:42:3], BM, float(C - 1), A.min, -1.0, A.add, r="bm", w="ff0")
    tt(T.g4[:], T.kr[:].indirect(T.obr[:]), T.m16[:], A.mult, KR + " obr0 obr1 m16", "g4")
    hold(T.g3[:], T.r16[:], T.g4[:], "r16 g4", "g3")

    def unpack(k):
        for b in range(4):
            mm(BK[k] + b, 128, *E(b), T.ly[:, LO[k]:LO[k] + 128], T.lys[:, LO[k]:LO[k] + 128], "qe%d ly0 lys0 ly%d lys%d" % (b, k, k), True, False)

    def place(k):
        a, e = NEW[k], LO[k] + 128
        c, d = a // 16, e // 16
        tt(T.ff[:, 3 * c + 1:3 * d:3], T.ls[:, c:d], T.g3[:, a + 15:e:16], A.is_ge, "ls%d g3" % k, "ff1%d" % k)
        tt(T.ff[:, 3 * c + 2:3 * d:3], T.ls[:, c:d], T.g3[:, B + a + 15:B + e:16], A.is_gt, "ls%d g3" % k, "ff2%d" % k)
        hold(T.fp[:, 3 * c:3 * d], T.r3[:, 3 * c:3 * d], T.ff[:, 3 * c:3 * d], "r3 ff0 ff1%d ff2%d" % (k, k), "fp%d" % k)
        cp(T.opp[:, c:d], T.fp[:, 3 * c + 2:3 * d:3], "fp%d" % k, "opp%d" % k)

    def pick(k):
        a, e = NEW[k], LO[k] + 128
        for b in (0, 2, 1, 3):
            win, out = T.zt[:, SP * b:SP * b + C + 2].indirect(T.opp[:, a // 16:e // 16]), T.z2[:, 4 * a + b:4 * e:4]
            if b < 2:
                act(out, win, "zt ze0 ze1 opp%d" % k, "z2%d%d" % (k, b))
            else:
                cp(out, win, "zt ze0 ze1 opp%d" % k, "z2%d%d" % (k, b))

    def store(k):
        a, e, o = NEW[k], LO[k] + 128, 128 * k + NEW[k] - LO[k]
        pack("y2", k)
        mm(BK[k], 128, T.qv[:], T.sv[:], *half("y2", k), "qv qy2%d" % k)
        dma("y", "oc%d" % k, T.oc[:, 4 * a:4 * e], raw(T.qy2[:, o:128 * k + 128]), r="qy2%d" % k)
        for j in range(4):
            dma("s" if k else "y", "o%d%d" % (k, j), T.osc[4 * j:4 * j + 4, a:e], T.sy2[32 * j:32 * j + 4, o:128 * k + 128], r="qy2%d" % k)

    def store_y(k):
        a, e = NEW[k], LO[k] + 128
        cp(T.yo[:, a:e], P(BK[k], a - LO[k], 128), "", "yo%d" % k, "p%d" % BK[k])
        dma("y", "y%d" % k, T.y[:, a:e], T.yo[:, a:e], r="yo%d" % k)

    unpack(0)
    place(0)
    pick(0)
    layer("z2", 0)
    unpack(1)
    place(1)
    combine("y2", 0, (0,))
    pick(1)
    layer("z2", 1)
    combine("y2", 0, (2, 1, 3))
    act(T.ovr[:], T.iot[:].indirect(T.opp[:]), "iot opp0 opp1", "ovr")
    dma("y", "ov", T.ov[:], T.ovr[0:128:16, :], r="ovr")
    store(0)
    combine("y2", 1, (0, 2, 1, 3))
    store(1)
    store_y(0)
    store_y(1)

    for q in cnt:
        wait("g", ("c" + q, cnt[q]))
    wait("g", ("sent", sent[0]))
    for d in dmas:
        wait("g", (d, 16))
